import numpy as np
import ml_dtypes


def mxq(x, axis, fmt="e4m3"):
    dtype, down = {"e4m3": (ml_dtypes.float8_e4m3fn, 7), "e5m2": (ml_dtypes.float8_e5m2, 14)}[fmt]
    v = np.moveaxis(np.asarray(x, np.float32).astype(ml_dtypes.bfloat16).astype(np.float64), axis, -1)
    blocks = v.reshape(v.shape[:-1] + (-1, 32))
    amax = np.abs(blocks).max(-1, keepdims=True)
    byte = np.maximum(np.where(amax > 0, np.frexp(amax)[1] - 1 + 127, 0) - down, 1)
    scale = np.exp2(byte - 127.0)
    codes = (blocks / scale).astype(np.float32).astype(dtype).astype(np.float64)
    return np.moveaxis((codes * scale).reshape(v.shape), -1, axis)


WIDE = False


def mx_kscale(k):
    if not WIDE:
        return np.ones(k)
    levels = np.array([10, -10, 5, -5, 0])
    if k % 512:
        return np.exp2(np.random.permutation(np.resize(levels, k // 32))).repeat(32)
    a = np.empty((k // 512, 16))
    for p in range(k // 512):
        a[p, :8] = np.random.permutation(np.resize(levels, 8))
        for g in range(8):
            far = levels[np.abs(levels - a[p, g]) >= 10]
            a[p, g + 8] = far[np.random.randint(len(far))]
    return np.exp2(a.ravel()).repeat(32)


def f64(x):
    return np.asarray(x).astype(np.float64)


def striped(idx):
    return np.tile(idx.reshape(-1, 16).T, (8, 1)).astype(np.uint16)


def unstriped(offs):
    return offs[:16].T.reshape(-1).astype(np.int64)


def pack_weight(w):
    k, n = w.shape
    w = f64(np.asarray(w, np.float32).astype(ml_dtypes.bfloat16)).reshape(k // 32, 32, n)
    amax = np.abs(w).max(1)
    byte = np.clip(np.where(amax > 0, np.frexp(amax)[1] - 1 + 127 - 7, 1), 1, 254)
    scaled = (w * np.exp2(127.0 - byte)[:, None, :]).reshape(k, n).astype(np.float32)
    words = np.ascontiguousarray(scaled.reshape(k // 512, 128, 4, n).transpose(0, 1, 3, 2)).astype(ml_dtypes.float8_e4m3fn).view(np.uint8)
    return words, np.ascontiguousarray(byte.astype(np.uint8).reshape(k // 512, 16, n))


def unpack_weight(words, scales):
    g, p, n, _ = words.shape
    vals = np.ascontiguousarray(words).view(ml_dtypes.float8_e4m3fn).astype(np.float64) * np.repeat(np.exp2(scales.astype(np.float64) - 127.0), 8, axis=1)[..., None]
    return vals.transpose(0, 1, 3, 2).reshape(g * 512, n)


def silu(v):
    return v / (1.0 + np.exp(-np.maximum(v, -700.0)))


K, T, S, V, H, N, J, U = 512, 2048, 512, 256, 512, 256, 512, 512


def setup_inputs():
    n = np.random.standard_normal
    s = mx_kscale(K)[:, None]
    u = mx_kscale(H)
    r = mx_kscale(J)[:, None]
    packed_w2 = pack_weight(n((H, N)) / np.sqrt(2 * H) / u[:, None])
    return {
        "xT": (n((K, T)) * s).astype(np.float32),
        "aT": (n((J, U)) * r).astype(np.float32),
        "w1": (n((K, H)) / np.sqrt(K) / s * u).astype(np.float32),
        "w3": (n((J, H)) / np.sqrt(J) / r).astype(np.float32),
        "w2_words": packed_w2[0],
        "w2_scales": packed_w2[1],
        "offs": striped(np.random.permutation(T)[:S]),
        "pos1": striped(np.random.permutation(S)[:V]),
        "pos2": striped(np.random.permutation(S)[:V]),
    }


def reference(xT, aT, w1, w3, w2_words, w2_scales, offs, pos1, pos2):
    xq = mxq(f64(xT)[:, unstriped(offs)], 0, "e4m3")
    h = silu(mxq(f64(w1), 0, "e4m3").T @ xq)
    f = mxq(f64(w3), 0, "e4m3").T @ mxq(f64(aT), 0, "e4m3")
    z = h[:, unstriped(pos1)] * f[:, :V] + h[:, unstriped(pos2)] * f[:, V:2 * V]
    return silu(unpack_weight(w2_words, w2_scales).T @ mxq(z, 0, "e4m3"))

@@ -1,0 +1,214 @@
+from contextlib import ExitStack
+
+import concourse.mybir as mybir
+
+K, T, S, V, H, N = 512, 2048, 512, 256, 512, 256
+FLOPS = 2 * (K * H * S + K * H * S + H * N * V)
+
+F32 = mybir.dt.float32
+BF16 = mybir.dt.bfloat16
+I32 = mybir.dt.int32
+U32 = mybir.dt.uint32
+U16 = mybir.dt.uint16
+U8 = mybir.dt.uint8
+FP8X4 = mybir.dt.float8_e4m3fn_x4
+SILU = mybir.ActivationFunctionType.Silu
+MULT = mybir.AluOpType.mult
+ADD = mybir.AluOpType.add
+
+P = 128
+PACK = 4
+HALF_M = P // 2
+HALF_V = V // 2
+HALF_S = S // 2
+
+
+def tile_picked_dime_silu_e_kernel(
+    tc, xT, aT, w1, w3, w2_words, w2_scales, offs, pos1, pos2, out
+):
+    nc = tc.nc
+    with ExitStack() as ctx:
+        lists = ctx.enter_context(tc.tile_pool(name="lists", bufs=1))
+        sb = ctx.enter_context(tc.tile_pool(name="sb", bufs=1))
+        psum = ctx.enter_context(tc.psum_pool(name="psum", bufs=1))
+
+        def tile(shape, dtype, name):
+            return sb.tile(shape, dtype, name=name, align_bytes=64)
+
+        def quantize(codes, scales, values):
+            nc.vector.quantize_mx(out=codes.bitcast(FP8X4), scales=scales, in_=values)
+
+        def product(acc, w_codes, w_scales, codes, scales):
+            nc.tensor.matmul_mx(
+                out=acc, lhsT=w_codes.bitcast(FP8X4), lhsT_scale=w_scales,
+                rhs=codes.bitcast(FP8X4), rhs_scale=scales, start=True, stop=True,
+            )
+
+        offs_sb = lists.tile([P, S // 16], U16, name="offs_sb")
+        pos_sb = [lists.tile([P, V // 16], U16, name=f"pos_sb{d}") for d in range(2)]
+
+        w2_scale_sb = tile([P, N], U8, "w2_scale_sb")
+        nc.vector.memset(w2_scale_sb[:].bitcast(I32), 0)
+
+        warm = tile([P, 1], F32, "warm")
+        warm_out = tile([P, 1], F32, "warm_out")
+        nc.vector.memset(warm[:], 0.0)
+        nc.scalar.activation(out=warm_out[:], in_=warm[:], func=SILU)
+
+        w3_raw = tile([P, PACK, H], F32, "w3_raw")
+        nc.sync.dma_start(out=w3_raw[:], in_=w3.rearrange("(p j) c -> p j c", j=PACK))
+        a_rows = aT.rearrange("(p j) c -> p j c", j=PACK)
+        a_raw = [tile([P, PACK, V], F32, f"a_raw{d}") for d in range(2)]
+        nc.sync.dma_start(out=a_raw[0][:], in_=a_rows[:, :, 0:V])
+        x_rows = xT.rearrange("(p j) c -> p j c", j=PACK)
+        x_raw = [tile([P, T], F32, f"x_raw{j}") for j in range(PACK)]
+        nc.sync.dma_start(out=x_raw[0][:], in_=x_rows[:, 0, :])
+        nc.sync.dma_start(offs_sb[:], offs)
+        for j in range(1, PACK):
+            nc.sync.dma_start(out=x_raw[j][:], in_=x_rows[:, j, :])
+        w1_rows = w1.rearrange("(p j) c -> p j c", j=PACK)
+        w1_raw = [tile([P, PACK, H // 2], F32, f"w1_raw{u}") for u in range(2)]
+        for u in range(2):
+            nc.sync.dma_start(out=w1_raw[u][:], in_=w1_rows[:, :, u * (H // 2) : (u + 1) * (H // 2)])
+        nc.sync.dma_start(out=a_raw[1][:], in_=a_rows[:, :, V : 2 * V])
+        nc.sync.dma_start(pos_sb[0][:], pos1)
+        nc.sync.dma_start(pos_sb[1][:], pos2)
+        w2_codes = tile([P, N], I32, "w2_codes")
+        nc.sync.dma_start(out=w2_codes[:], in_=w2_words[0].rearrange("p n t -> p (n t)").bitcast(I32))
+        w2_scale_rows = w2_scales[0].bitcast(I32)
+        for q in range(4):
+            nc.sync.dma_start(
+                out=w2_scale_sb[:].bitcast(I32)[32 * q : 32 * q + 4, :],
+                in_=w2_scale_rows[4 * q : 4 * q + 4, :],
+            )
+
+        w3_bf = tile([P, PACK, P, PACK], BF16, "w3_bf")
+        nc.scalar.copy(
+            out=w3_bf[:].rearrange("p t m j -> p m j t"),
+            in_=w3_raw[:].rearrange("p j (m t) -> p m j t", t=PACK),
+        )
+        w3_codes = tile([P, H], U32, "w3_codes")
+        w3_scales = tile([P, H], U8, "w3_scales")
+        quantize(w3_codes[:], w3_scales[:], w3_bf[:].rearrange("p t m j -> p (t m j)"))
+
+        a_bf = [tile([P, V, PACK], BF16, f"a_bf{d}") for d in range(2)]
+        a_codes = [tile([P, V], U32, f"a_codes{d}") for d in range(2)]
+        a_scales = [tile([P, V], U8, f"a_scales{d}") for d in range(2)]
+        f_sb = [[tile([P, 2, V], F32, f"f_sb{d}_{s}") for s in range(2)] for d in range(2)]
+
+        def round_angles(d, copy):
+            copy(
+                out=a_bf[d][:].rearrange("p (c i) j -> p c j i", i=4),
+                in_=a_raw[d][:].rearrange("p j (c i) -> p c j i", i=4),
+            )
+
+        def filters(d):
+            quantize(a_codes[d][:], a_scales[d][:], a_bf[d][:].rearrange("p v j -> p (v j)"))
+            for s in range(2):
+                bank = psum.tile([P, 2, V], F32, name=f"f_bank{d}_{s}", tag=f"f_bank{d}_{s}")
+                for e in range(2):
+                    cols = slice((2 * s + e) * P, (2 * s + e + 1) * P)
+                    product(bank[:, e, :], w3_codes[:, cols], w3_scales[:, cols], a_codes[d][:], a_scales[d][:])
+                nc.scalar.copy(out=f_sb[d][s][:], in_=bank[:])
+
+        round_angles(0, nc.scalar.copy)
+        filters(0)
+
+        x_bf = tile([P, S, PACK], BF16, "x_bf")
+        for j in range(PACK - 1):
+            nc.vector.tensor_copy(out=x_bf[:, :, j], in_=x_raw[j][:].indirect(offs_sb[:]))
+        halves = [slice(u * HALF_S, (u + 1) * HALF_S) for u in range(2)]
+        for u in range(2):
+            nc.vector.tensor_copy(
+                out=x_bf[:, halves[u], PACK - 1],
+                in_=x_raw[PACK - 1][:].indirect(offs_sb[:, u * (HALF_S // 16) : (u + 1) * (HALF_S // 16)]),
+            )
+        x_codes = tile([P, S], U32, "x_codes")
+        x_scales = tile([P, S], U8, "x_scales")
+        for u in range(2):
+            quantize(x_codes[:, halves[u]], x_scales[:, halves[u]], x_bf[:, halves[u], :].rearrange("p s j -> p (s j)"))
+
+        w1_bf = [tile([P, 2, P, PACK], BF16, f"w1_bf{s}") for s in range(2)]
+
+        def round_w1(u, s, copy):
+            copy(
+                out=w1_bf[s][:, :, u * HALF_M : (u + 1) * HALF_M, :].rearrange("p e m j -> p m j e"),
+                in_=w1_raw[u][:].rearrange("p j (m s e) -> p s m j e", s=2, e=2)[:, s],
+            )
+
+        round_w1(0, 0, nc.scalar.copy)
+        round_w1(0, 1, nc.scalar.copy)
+        round_w1(1, 0, nc.scalar.copy)
+        round_w1(1, 1, nc.vector.tensor_copy)
+
+        h_sb = []
+        for t in range(PACK):
+            codes = tile([P, P], U32, f"w1_codes{t}")
+            scales = tile([P, P], U8, f"w1_scales{t}")
+            quantize(codes[:], scales[:], w1_bf[t // 2][:, t % 2].rearrange("p m j -> p (m j)"))
+            h_t = tile([P, S], F32, f"h_sb{t}")
+            if t == 0:
+                for u in range(2):
+                    bank = psum.tile([P, 2, V], F32, name=f"h_bank0_{u}", tag=f"f_bank0_{u}")
+                    product(bank[:, 0, :], codes[:], scales[:], x_codes[:, halves[u]], x_scales[:, halves[u]])
+                    nc.scalar.activation(out=h_t[:, halves[u]], in_=bank[:, 0, :], func=SILU)
+            else:
+                bank = psum.tile([P, S], F32, name=f"h_bank{t}", tag=f"h_bank{t}")
+                product(bank[:], codes[:], scales[:], x_codes[:], x_scales[:])
+                nc.scalar.activation(out=h_t[:], in_=bank[:], func=SILU)
+            h_sb.append(h_t)
+
+        round_angles(1, nc.vector.tensor_copy)
+        filters(1)
+
+        first = tile([P, PACK, V], F32, "first")
+        for t in range(PACK):
+            nc.vector.tensor_tensor(
+                first[:, t, :], h_sb[t][:].indirect(pos_sb[0][:]), f_sb[0][t // 2][:, t % 2, :], MULT
+            )
+        out_rows = out.rearrange("(g p) v -> p g v", p=P)
+        cols = [slice(r * HALF_V, (r + 1) * HALF_V) for r in range(2)]
+        second = [tile([P, PACK, HALF_V], F32, f"second{r}") for r in range(2)]
+        z_bf = [tile([P, HALF_V, PACK], BF16, f"z_bf{r}") for r in range(2)]
+
+        def second_term(r, t):
+            nc.vector.tensor_tensor(
+                second[r][:, t, :],
+                h_sb[t][:].indirect(pos_sb[1][:, r * (HALF_V // 16) : (r + 1) * (HALF_V // 16)]),
+                f_sb[1][t // 2][:, t % 2, cols[r]],
+                MULT,
+            )
+
+        def add_terms(r):
+            nc.vector.tensor_tensor(
+                z_bf[r][:].rearrange("p (c i) t -> p c t i", i=4),
+                first[:, :, cols[r]].rearrange("p t (c i) -> p c t i", i=4),
+                second[r][:].rearrange("p t (c i) -> p c t i", i=4),
+                ADD,
+            )
+
+        def project(r):
+            z_codes = tile([P, HALF_V], U32, f"z_codes{r}")
+            z_scales = tile([P, HALF_V], U8, f"z_scales{r}")
+            quantize(z_codes[:], z_scales[:], z_bf[r][:].rearrange("p v t -> p (v t)"))
+            bank = psum.tile([P, 2, V], F32, name=f"out_bank{r}", tag=f"f_bank0_{r}")
+            for g in range(2):
+                rows = slice(g * P, (g + 1) * P)
+                product(
+                    bank[:, 0, g * HALF_V : (g + 1) * HALF_V],
+                    w2_codes[:, rows].bitcast(U32), w2_scale_sb[:, rows], z_codes[:], z_scales[:],
+                )
+            result = tile([P, 2, HALF_V], F32, f"result{r}")
+            nc.scalar.activation(out=result[:].rearrange("p g v -> p (g v)"), in_=bank[:, 0, :], func=SILU)
+            nc.scalar.dma_start(out=out_rows[:, :, cols[r]], in_=result[:])
+
+        for t in range(PACK):
+            second_term(0, t)
+        second_term(1, 0)
+        add_terms(0)
+        second_term(1, 1)
+        project(0)
+        second_term(1, 2)
+        second_term(1, 3)
+        add_terms(1)
+        project(1)

@@ -64,6 +64,8 @@ def tile_picked_dime_silu_e_kernel(
         x_raw = [tile([P, T], F32, f"x_raw{j}") for j in range(PACK)]
         nc.sync.dma_start(out=x_raw[0][:], in_=x_rows[:, 0, :])
         nc.sync.dma_start(offs_sb[:], offs)
+        nc.sync.dma_start(pos_sb[0][:], pos1)
+        nc.sync.dma_start(pos_sb[1][:], pos2)
         for j in range(1, PACK):
             nc.sync.dma_start(out=x_raw[j][:], in_=x_rows[:, j, :])
         w1_rows = w1.rearrange("(p j) c -> p j c", j=PACK)
@@ -71,8 +73,6 @@ def tile_picked_dime_silu_e_kernel(
         for u in range(2):
             nc.sync.dma_start(out=w1_raw[u][:], in_=w1_rows[:, :, u * (H // 2) : (u + 1) * (H // 2)])
         nc.sync.dma_start(out=a_raw[1][:], in_=a_rows[:, :, V : 2 * V])
-        nc.sync.dma_start(pos_sb[0][:], pos1)
-        nc.sync.dma_start(pos_sb[1][:], pos2)
         w2_codes = tile([P, N], I32, "w2_codes")
         nc.sync.dma_start(out=w2_codes[:], in_=w2_words[0].rearrange("p n t -> p (n t)").bitcast(I32))
         w2_scale_rows = w2_scales[0].bitcast(I32)
@@ -139,7 +139,7 @@ def tile_picked_dime_silu_e_kernel(
         round_w1(0, 0, nc.scalar.copy)
         round_w1(0, 1, nc.scalar.copy)
         round_w1(1, 0, nc.scalar.copy)
-        round_w1(1, 1, nc.vector.tensor_copy)
+        round_w1(1, 1, nc.scalar.copy)
 
         h_sb = []
         for t in range(PACK):
@@ -168,14 +168,14 @@ def tile_picked_dime_silu_e_kernel(
             )
         out_rows = out.rearrange("(g p) v -> p g v", p=P)
         cols = [slice(r * HALF_V, (r + 1) * HALF_V) for r in range(2)]
-        second = [tile([P, PACK, HALF_V], F32, f"second{r}") for r in range(2)]
+        second = tile([P, PACK, V], F32, "second")
         z_bf = [tile([P, HALF_V, PACK], BF16, f"z_bf{r}") for r in range(2)]
 
-        def second_term(r, t):
+        def second_term(t, c):
             nc.vector.tensor_tensor(
-                second[r][:, t, :],
-                h_sb[t][:].indirect(pos_sb[1][:, r * (HALF_V // 16) : (r + 1) * (HALF_V // 16)]),
-                f_sb[1][t // 2][:, t % 2, cols[r]],
+                second[:, t, c],
+                h_sb[t][:].indirect(pos_sb[1][:, c.start // 16 : c.stop // 16]),
+                f_sb[1][t // 2][:, t % 2, c],
                 MULT,
             )
 
@@ -183,11 +183,11 @@ def tile_picked_dime_silu_e_kernel(
             nc.vector.tensor_tensor(
                 z_bf[r][:].rearrange("p (c i) t -> p c t i", i=4),
                 first[:, :, cols[r]].rearrange("p t (c i) -> p c t i", i=4),
-                second[r][:].rearrange("p t (c i) -> p c t i", i=4),
+                second[:, :, cols[r]].rearrange("p t (c i) -> p c t i", i=4),
                 ADD,
             )
 
-        def project(r):
+        def project(r, store_queue):
             z_codes = tile([P, HALF_V], U32, f"z_codes{r}")
             z_scales = tile([P, HALF_V], U8, f"z_scales{r}")
             quantize(z_codes[:], z_scales[:], z_bf[r][:].rearrange("p v t -> p (v t)"))
@@ -200,15 +200,13 @@ def tile_picked_dime_silu_e_kernel(
                 )
             result = tile([P, 2, HALF_V], F32, f"result{r}")
             nc.scalar.activation(out=result[:].rearrange("p g v -> p (g v)"), in_=bank[:, 0, :], func=SILU)
-            nc.scalar.dma_start(out=out_rows[:, :, cols[r]], in_=result[:])
+            store_queue.dma_start(out=out_rows[:, :, cols[r]], in_=result[:])
 
-        for t in range(PACK):
-            second_term(0, t)
-        second_term(1, 0)
-        add_terms(0)
-        second_term(1, 1)
-        project(0)
-        second_term(1, 2)
-        second_term(1, 3)
-        add_terms(1)
-        project(1)
+        for t in range(PACK - 1):
+            second_term(t, slice(0, V))
+        for r in range(2):
+            second_term(PACK - 1, cols[r])
+        for r in range(2):
+            add_terms(r)
+        project(0, nc.sync)
+        project(1, nc.scalar)

from contextlib import ExitStack

import concourse.mybir as mybir

K, T, S, V, H, N = 512, 2048, 512, 256, 512, 256
FLOPS = 2 * (K * H * S + K * H * S + H * N * V)

F32 = mybir.dt.float32
BF16 = mybir.dt.bfloat16
I32 = mybir.dt.int32
U32 = mybir.dt.uint32
U16 = mybir.dt.uint16
U8 = mybir.dt.uint8
FP8X4 = mybir.dt.float8_e4m3fn_x4
SILU = mybir.ActivationFunctionType.Silu
MULT = mybir.AluOpType.mult
ADD = mybir.AluOpType.add

P = 128
PACK = 4
HALF_M = P // 2
HALF_V = V // 2
HALF_S = S // 2


def tile_picked_dime_silu_e_kernel(
    tc, xT, aT, w1, w3, w2_words, w2_scales, offs, pos1, pos2, out
):
    nc = tc.nc
    with ExitStack() as ctx:
        lists = ctx.enter_context(tc.tile_pool(name="lists", bufs=1))
        sb = ctx.enter_context(tc.tile_pool(name="sb", bufs=1))
        psum = ctx.enter_context(tc.psum_pool(name="psum", bufs=1))

        def tile(shape, dtype, name):
            return sb.tile(shape, dtype, name=name, align_bytes=64)

        def quantize(codes, scales, values):
            nc.vector.quantize_mx(out=codes.bitcast(FP8X4), scales=scales, in_=values)

        def product(acc, w_codes, w_scales, codes, scales):
            nc.tensor.matmul_mx(
                out=acc, lhsT=w_codes.bitcast(FP8X4), lhsT_scale=w_scales,
                rhs=codes.bitcast(FP8X4), rhs_scale=scales, start=True, stop=True,
            )

        offs_sb = lists.tile([P, S // 16], U16, name="offs_sb")
        pos_sb = [lists.tile([P, V // 16], U16, name=f"pos_sb{d}") for d in range(2)]

        w2_scale_sb = tile([P, N], U8, "w2_scale_sb")
        nc.vector.memset(w2_scale_sb[:].bitcast(I32), 0)

        warm = tile([P, 1], F32, "warm")
        warm_out = tile([P, 1], F32, "warm_out")
        nc.vector.memset(warm[:], 0.0)
        nc.scalar.activation(out=warm_out[:], in_=warm[:], func=SILU)

        w3_raw = tile([P, PACK, H], F32, "w3_raw")
        nc.sync.dma_start(out=w3_raw[:], in_=w3.rearrange("(p j) c -> p j c", j=PACK))
        a_rows = aT.rearrange("(p j) c -> p j c", j=PACK)
        a_raw = [tile([P, PACK, V], F32, f"a_raw{d}") for d in range(2)]
        nc.sync.dma_start(out=a_raw[0][:], in_=a_rows[:, :, 0:V])
        x_rows = xT.rearrange("(p j) c -> p j c", j=PACK)
        x_raw = [tile([P, T], F32, f"x_raw{j}") for j in range(PACK)]
        nc.sync.dma_start(out=x_raw[0][:], in_=x_rows[:, 0, :])
        nc.sync.dma_start(offs_sb[:], offs)
        nc.sync.dma_start(pos_sb[0][:], pos1)
        nc.sync.dma_start(pos_sb[1][:], pos2)
        for j in range(1, PACK):
            nc.sync.dma_start(out=x_raw[j][:], in_=x_rows[:, j, :])
        w1_rows = w1.rearrange("(p j) c -> p j c", j=PACK)
        w1_raw = [tile([P, PACK, H // 2], F32, f"w1_raw{u}") for u in range(2)]
        for u in range(2):
            nc.sync.dma_start(out=w1_raw[u][:], in_=w1_rows[:, :, u * (H // 2) : (u + 1) * (H // 2)])
        nc.sync.dma_start(out=a_raw[1][:], in_=a_rows[:, :, V : 2 * V])
        w2_codes = tile([P, N], I32, "w2_codes")
        nc.sync.dma_start(out=w2_codes[:], in_=w2_words[0].rearrange("p n t -> p (n t)").bitcast(I32))
        w2_scale_rows = w2_scales[0].bitcast(I32)
        for q in range(4):
            nc.sync.dma_start(
                out=w2_scale_sb[:].bitcast(I32)[32 * q : 32 * q + 4, :],
                in_=w2_scale_rows[4 * q : 4 * q + 4, :],
            )

        w3_bf = tile([P, PACK, P, PACK], BF16, "w3_bf")
        nc.scalar.copy(
            out=w3_bf[:].rearrange("p t m j -> p m j t"),
            in_=w3_raw[:].rearrange("p j (m t) -> p m j t", t=PACK),
        )
        w3_codes = tile([P, H], U32, "w3_codes")
        w3_scales = tile([P, H], U8, "w3_scales")
        quantize(w3_codes[:], w3_scales[:], w3_bf[:].rearrange("p t m j -> p (t m j)"))

        a_bf = [tile([P, V, PACK], BF16, f"a_bf{d}") for d in range(2)]
        a_codes = [tile([P, V], U32, f"a_codes{d}") for d in range(2)]
        a_scales = [tile([P, V], U8, f"a_scales{d}") for d in range(2)]
        f_sb = [[tile([P, 2, V], F32, f"f_sb{d}_{s}") for s in range(2)] for d in range(2)]

        def round_angles(d, copy):
            copy(
                out=a_bf[d][:].rearrange("p (c i) j -> p c j i", i=4),
                in_=a_raw[d][:].rearrange("p j (c i) -> p c j i", i=4),
            )

        def filters(d):
            quantize(a_codes[d][:], a_scales[d][:], a_bf[d][:].rearrange("p v j -> p (v j)"))
            for s in range(2):
                bank = psum.tile([P, 2, V], F32, name=f"f_bank{d}_{s}", tag=f"f_bank{d}_{s}")
                for e in range(2):
                    cols = slice((2 * s + e) * P, (2 * s + e + 1) * P)
                    product(bank[:, e, :], w3_codes[:, cols], w3_scales[:, cols], a_codes[d][:], a_scales[d][:])
                nc.scalar.copy(out=f_sb[d][s][:], in_=bank[:])

        round_angles(0, nc.scalar.copy)
        filters(0)

        x_bf = tile([P, S, PACK], BF16, "x_bf")
        for j in range(PACK - 1):
            nc.vector.tensor_copy(out=x_bf[:, :, j], in_=x_raw[j][:].indirect(offs_sb[:]))
        halves = [slice(u * HALF_S, (u + 1) * HALF_S) for u in range(2)]
        for u in range(2):
            nc.vector.tensor_copy(
                out=x_bf[:, halves[u], PACK - 1],
                in_=x_raw[PACK - 1][:].indirect(offs_sb[:, u * (HALF_S // 16) : (u + 1) * (HALF_S // 16)]),
            )
        x_codes = tile([P, S], U32, "x_codes")
        x_scales = tile([P, S], U8, "x_scales")
        for u in range(2):
            quantize(x_codes[:, halves[u]], x_scales[:, halves[u]], x_bf[:, halves[u], :].rearrange("p s j -> p (s j)"))

        w1_bf = [tile([P, 2, P, PACK], BF16, f"w1_bf{s}") for s in range(2)]

        def round_w1(u, s, copy):
            copy(
                out=w1_bf[s][:, :, u * HALF_M : (u + 1) * HALF_M, :].rearrange("p e m j -> p m j e"),
                in_=w1_raw[u][:].rearrange("p j (m s e) -> p s m j e", s=2, e=2)[:, s],
            )

        round_w1(0, 0, nc.scalar.copy)
        round_w1(0, 1, nc.scalar.copy)
        round_w1(1, 0, nc.scalar.copy)
        round_w1(1, 1, nc.scalar.copy)

        h_sb = []
        for t in range(PACK):
            codes = tile([P, P], U32, f"w1_codes{t}")
            scales = tile([P, P], U8, f"w1_scales{t}")
            quantize(codes[:], scales[:], w1_bf[t // 2][:, t % 2].rearrange("p m j -> p (m j)"))
            h_t = tile([P, S], F32, f"h_sb{t}")
            if t == 0:
                for u in range(2):
                    bank = psum.tile([P, 2, V], F32, name=f"h_bank0_{u}", tag=f"f_bank0_{u}")
                    product(bank[:, 0, :], codes[:], scales[:], x_codes[:, halves[u]], x_scales[:, halves[u]])
                    nc.scalar.activation(out=h_t[:, halves[u]], in_=bank[:, 0, :], func=SILU)
            else:
                bank = psum.tile([P, S], F32, name=f"h_bank{t}", tag=f"h_bank{t}")
                product(bank[:], codes[:], scales[:], x_codes[:], x_scales[:])
                nc.scalar.activation(out=h_t[:], in_=bank[:], func=SILU)
            h_sb.append(h_t)

        round_angles(1, nc.vector.tensor_copy)
        filters(1)

        first = tile([P, PACK, V], F32, "first")
        for t in range(PACK):
            nc.vector.tensor_tensor(
                first[:, t, :], h_sb[t][:].indirect(pos_sb[0][:]), f_sb[0][t // 2][:, t % 2, :], MULT
            )
        out_rows = out.rearrange("(g p) v -> p g v", p=P)
        cols = [slice(r * HALF_V, (r + 1) * HALF_V) for r in range(2)]
        second = tile([P, PACK, V], F32, "second")
        z_bf = [tile([P, HALF_V, PACK], BF16, f"z_bf{r}") for r in range(2)]

        def second_term(t, c):
            nc.vector.tensor_tensor(
                second[:, t, c],
                h_sb[t][:].indirect(pos_sb[1][:, c.start // 16 : c.stop // 16]),
                f_sb[1][t // 2][:, t % 2, c],
                MULT,
            )

        def add_terms(r):
            nc.vector.tensor_tensor(
                z_bf[r][:].rearrange("p (c i) t -> p c t i", i=4),
                first[:, :, cols[r]].rearrange("p t (c i) -> p c t i", i=4),
                second[:, :, cols[r]].rearrange("p t (c i) -> p c t i", i=4),
                ADD,
            )

        def project(r, store_queue):
            z_codes = tile([P, HALF_V], U32, f"z_codes{r}")
            z_scales = tile([P, HALF_V], U8, f"z_scales{r}")
            quantize(z_codes[:], z_scales[:], z_bf[r][:].rearrange("p v t -> p (v t)"))
            bank = psum.tile([P, 2, V], F32, name=f"out_bank{r}", tag=f"f_bank0_{r}")
            for g in range(2):
                rows = slice(g * P, (g + 1) * P)
                product(
                    bank[:, 0, g * HALF_V : (g + 1) * HALF_V],
                    w2_codes[:, rows].bitcast(U32), w2_scale_sb[:, rows], z_codes[:], z_scales[:],
                )
            result = tile([P, 2, HALF_V], F32, f"result{r}")
            nc.scalar.activation(out=result[:].rearrange("p g v -> p (g v)"), in_=bank[:, 0, :], func=SILU)
            store_queue.dma_start(out=out_rows[:, :, cols[r]], in_=result[:])

        for t in range(PACK - 1):
            second_term(t, slice(0, V))
        for r in range(2):
            second_term(PACK - 1, cols[r])
        for r in range(2):
            add_terms(r)
        project(0, nc.sync)
        project(1, nc.scalar)
